import numpy as np
import ml_dtypes


def mxq(x, axis, fmt="e4m3"):
    dtype, down = {"e4m3": (ml_dtypes.float8_e4m3fn, 7), "e5m2": (ml_dtypes.float8_e5m2, 14)}[fmt]
    v = np.moveaxis(np.asarray(x, np.float32).astype(ml_dtypes.bfloat16).astype(np.float64), axis, -1)
    blocks = v.reshape(v.shape[:-1] + (-1, 32))
    amax = np.abs(blocks).max(-1, keepdims=True)
    byte = np.maximum(np.where(amax > 0, np.frexp(amax)[1] - 1 + 127, 0) - down, 1)
    scale = np.exp2(byte - 127.0)
    codes = (blocks / scale).astype(np.float32).astype(dtype).astype(np.float64)
    return np.moveaxis((codes * scale).reshape(v.shape), -1, axis)


WIDE = False


def mx_kscale(k):
    if not WIDE:
        return np.ones(k)
    levels = np.array([10, -10, 5, -5, 0])
    if k % 512:
        return np.exp2(np.random.permutation(np.resize(levels, k // 32))).repeat(32)
    a = np.empty((k // 512, 16))
    for p in range(k // 512):
        a[p, :8] = np.random.permutation(np.resize(levels, 8))
        for g in range(8):
            far = levels[np.abs(levels - a[p, g]) >= 10]
            a[p, g + 8] = far[np.random.randint(len(far))]
    return np.exp2(a.ravel()).repeat(32)


BF16 = ml_dtypes.bfloat16


def bf(x):
    return np.asarray(x, np.float32).astype(BF16)


def f64(x):
    return np.asarray(x).astype(np.float64)


E2M1 = np.array([0.0, 0.5, 1.0, 1.5, 2.0, 3.0, 4.0, 6.0, -0.0, -0.5, -1.0, -1.5, -2.0, -3.0, -4.0, -6.0])


def pack_weight(w, fmt):
    k, n = w.shape
    w = f64(bf(w)).reshape(k // 32, 32, n)
    amax = np.abs(w).max(1)
    if fmt == "e4m3":
        byte = np.frexp(amax)[1] - 1 + 127 - 7
    else:
        mant, ex = np.frexp(amax / 6.0)
        byte = np.where(mant > 0.5, ex, ex - 1) + 127
    byte = np.clip(np.where(amax > 0, byte, 1), 1, 254)
    scaled = (w * np.exp2(127.0 - byte)[:, None, :]).reshape(k, n).astype(np.float32)
    by_word = np.ascontiguousarray(scaled.reshape(k // 512, 128, 4, n).transpose(0, 1, 3, 2))
    if fmt == "e4m3":
        words = by_word.astype(ml_dtypes.float8_e4m3fn).view(np.uint8)
    else:
        c = by_word.astype(ml_dtypes.float4_e2m1fn).view(np.uint8) & 0xF
        words = c[..., 0::2] | (c[..., 1::2] << 4)
    return np.ascontiguousarray(words), np.ascontiguousarray(byte.astype(np.uint8).reshape(k // 512, 16, n))


def unpack_weight(words, scales, fmt):
    g, p, n, _ = words.shape
    if fmt == "e4m3":
        vals = np.ascontiguousarray(words).view(ml_dtypes.float8_e4m3fn).astype(np.float64)
    else:
        nib = np.empty((g, p, n, 4), np.uint8)
        nib[..., 0::2] = words & 0xF
        nib[..., 1::2] = words >> 4
        vals = E2M1[nib]
    vals = vals * np.repeat(np.exp2(scales.astype(np.float64) - 127.0), 8, axis=1)[..., None]
    return vals.transpose(0, 1, 3, 2).reshape(g * 512, n)
def pack4(w):
    words, scales = pack_weight(w, "e2m1")
    return words.reshape(words.shape[0], 128, -1), scales


def unpack4(words, scales):
    return unpack_weight(words.reshape(words.shape[0], 128, -1, 2), scales, "e2m1")


E4M3FN = np.array([(-1.0 if i & 128 else 1.0) * ((1.0 + (i & 7) / 8.0) * 2.0 ** (((i >> 3) & 15) - 7) if i & 120 else (i & 7) * 2.0 ** -9) for i in range(256)])


def e4m3fn_bytes(y):
    return np.clip(np.asarray(y, np.float64), -448.0, 448.0).astype(np.float32).astype(ml_dtypes.float8_e4m3fn).view(np.uint8)


def e4m3fn_values(b):
    return E4M3FN[b]


B, N, R = 1024, 1024, 1024
R2 = 2 * R


def soft_sign(u):
    return -1.0 + np.maximum(u + 1.0, 0.0) - np.maximum(u - 1.0, 0.0)


def draw0():
    a = mx_kscale(N)
    t = mx_kscale(R2)
    x = bf(np.random.standard_normal((B, N)) * a)
    v = bf(np.random.standard_normal((B, R)))
    hty = bf(np.random.standard_normal((B, R)))
    gram = bf(np.random.standard_normal((N, R)) / np.sqrt(N) / a[:, None])
    g = bf((1.0 + 0.1 * np.random.standard_normal(R2)) * t)
    words, scales = pack4(np.random.standard_normal((R2, N)) * 0.7 / np.sqrt(R2) / t[:, None])
    s = bf(np.random.uniform(0.3, 0.9, N) / a)
    return {
        "x": x,
        "v": v,
        "hty": hty,
        "gram": gram,
        "g": g,
        "w_words": words,
        "w_scales": scales,
        "s": s,
    }


def core(x, v, hty, gram, g, w_words, w_scales, s):
    x, v, hty, gram = f64(x), f64(v), f64(hty), f64(gram)
    g, s = f64(g), f64(s)
    gx = mxq(x, 1, "e4m3") @ mxq(gram, 0, "e4m3")
    r = hty - gx
    c = np.concatenate([r, v], axis=-1)
    cg = g[None, :] * c
    p = mxq(cg, 1, "e4m3") @ unpack4(w_words, w_scales)
    u = s[None, :] * x + p
    return soft_sign(u)


def setup_inputs():
    drawn = draw0()
    full = np.asarray(drawn['gram']).astype(np.float64)
    scale = (np.abs(full).reshape(1024, 8, 128).max(axis=(2,)) / 448.0).astype(np.float32)
    given = {}
    for key, value in drawn.items():
        if key == 'gram':
            given['gram_bytes'] = e4m3fn_bytes(full / np.repeat(scale.astype(np.float64), 128, axis=1))
            given['gram_scale'] = scale
        else:
            given[key] = value
    return given


def reference(x, v, hty, gram_bytes, gram_scale, g, w_words, w_scales, s):
    return core(x, v, hty, e4m3fn_values(gram_bytes) * np.repeat(gram_scale.astype(np.float64), 128, axis=1), g, w_words, w_scales, s)

@@ -1,0 +1,407 @@
+import concourse.mybir as mybir
+from concourse.masks import make_identity
+
+B, N, R = 1024, 1024, 1024
+FLOPS = 2 * B * N * R + 2 * B * (2 * R) * N
+
+F32 = mybir.dt.float32
+BF16 = mybir.dt.bfloat16
+I32 = mybir.dt.int32
+U32 = mybir.dt.uint32
+U8 = mybir.dt.uint8
+FP8 = mybir.dt.float8_e4m3fn
+FP8X4 = mybir.dt.float8_e4m3fn_x4
+FP4X4 = mybir.dt.float4_e2m1fn_x4
+ALU = mybir.AluOpType
+ACT = mybir.ActivationFunctionType
+P = 128
+DIAG = (4, 5, 6, 7)
+
+
+def tile_clippedlinearresidualupdate_kernel(
+    tc, x, v, hty, gram_bytes, gram_scale, g, w_words, w_scales, s, out
+):
+    nc = tc.nc
+    with tc.tile_pool(name="keep", bufs=1) as keep, tc.tile_pool(name="work", bufs=2) as work, tc.psum_pool(
+        name="psum", bufs=8
+    ) as psum:
+        gsc = keep.tile([P, 2, 32], F32, name="gsc")
+        nc.sync.dma_start(out=gsc[:], in_=gram_scale.rearrange("(g p t) j -> p g (t j)", p=P, t=4))
+        s_b = keep.tile([P, N], BF16, name="s_b")
+        gcol = keep.tile([P, 8], BF16, name="gcol")
+        scol = keep.tile([P, 8], BF16, name="scol")
+        g_b = keep.tile([P, R], BF16, name="g_b")
+        gview = gram_bytes.rearrange("(g p t) n -> g p t n", p=P, t=4)
+        graw = []
+        for a in range(2):
+            t_ = keep.tile([P, 4, N], U8, name="gram_raw%d" % a)
+            graw.append(t_)
+
+        def load_rows(src, label, tiles, rows):
+            for i in rows:
+                t_ = keep.tile([P, 1024], BF16, name="%s%d" % (label, i), align_bytes=64)
+                nc.sync.dma_start(out=t_[:], in_=src[P * i : P * i + P, :])
+                tiles.append(t_)
+
+        xt, ht, vt = [], [], []
+        nc.sync.dma_start(out=graw[0][:], in_=gview[0])
+        nc.scalar.dma_start(
+            out=gcol[:].rearrange("p (q t) -> p q t", t=4), in_=g[0:R].rearrange("(q p t) -> p q t", p=P, t=4)
+        )
+        nc.scalar.dma_start(
+            out=scol[:].rearrange("p (q t) -> p q t", t=4), in_=s.rearrange("(q p t) -> p q t", p=P, t=4)
+        )
+        nc.scalar.dma_start(out=s_b[:], in_=s.partition_broadcast(P))
+        load_rows(x, "x", xt, range(4))
+        nc.sync.dma_start(out=graw[1][:], in_=gview[1])
+        load_rows(x, "x", xt, range(4, 8))
+        load_rows(hty, "h", ht, range(8))
+        nc.sync.dma_start(out=g_b[:], in_=g[R : 2 * R].partition_broadcast(P))
+        for i in range(4):
+            t_ = keep.tile([P, 2, R], BF16, name="v%d" % i, align_bytes=64)
+            nc.sync.dma_start(out=t_[:], in_=v[2 * P * i : 2 * P * i + 2 * P, :].rearrange("(i p) n -> p i n", p=P))
+            vt.append(t_)
+
+        ident = keep.tile([P, P], F32, name="ident")
+        make_identity(nc, ident[:])
+        ident_b = keep.tile([P, P], BF16, name="ident_b")
+        make_identity(nc, ident_b[:])
+        diag = keep.tile([P, 8, P], BF16, name="diag")
+        nc.gpsimd.tensor_tensor(
+            out=diag[:],
+            in0=ident_b[:].unsqueeze(1).to_broadcast([P, 8, P]),
+            in1=scol[:].unsqueeze(2).to_broadcast([P, 8, P]),
+            op=ALU.mult,
+        )
+        ws = keep.tile([P, 4, N], U8, name="ws", align_bytes=64)
+        nc.gpsimd.memset(ws[:].bitcast(I32), 0)
+
+        w_sb = keep.tile([P, 4, 2 * N], U8, name="w_sb", align_bytes=64)
+        nc.sync.dma_start(out=w_sb[:], in_=w_words.rearrange("g p c -> p g c"))
+        for q in range(4):
+            nc.sync.dma_start(
+                out=ws[32 * q : 32 * q + 4, :, :].bitcast(I32),
+                in_=w_scales[:, 4 * q : 4 * q + 4, :].rearrange("g r n -> r g n").bitcast(I32),
+            )
+
+        gpos = keep.tile([P, 8], F32, name="gpos")
+        gneg = keep.tile([P, 8], F32, name="gneg")
+
+        def codes(label):
+            c = keep.tile([P, 512], U32, name=label + "_c", align_bytes=64)
+            sc = keep.tile([P, 512], U8, name=label + "_s", align_bytes=64)
+            return c[:], sc[:]
+
+        def bank():
+            b = psum.tile([P, 512], F32, name="bank", tag="bank")
+            return b
+
+        gp = {}
+        ggrp = {}
+        gq = {}
+
+        def gram_scale_cols(a, q):
+            t_ = work.tile([P, 4, 512], BF16, name="gp", tag="gp", bufs=2)
+            gp[a, q] = t_
+            for j in range(4):
+                for t in range(4):
+                    col = 512 * q + P * j
+                    k = 8 * t + 4 * q + j
+                    o = t_[:, t, P * j : P * j + P]
+                    i_ = graw[a][:, t, col : col + P].bitcast(FP8)
+                    sc = gsc[:, a, k : k + 1]
+                    if a == 0 and q == 0 and t >= 2:
+                        nc.vector.tensor_scalar(out=o, in0=i_, scalar1=sc, scalar2=None, op0=ALU.mult)
+                    else:
+                        nc.scalar.activation(out=o, in_=i_, func=ACT.Copy, scale=sc)
+
+        def gram_interleave(a, q):
+            t_ = work.tile([P, 2048], BF16, name="grp", tag="grp", bufs=3, align_bytes=64)
+            ggrp[a, q] = t_
+            nc.vector.tensor_copy(
+                out=t_[:].rearrange("p (tt m t) -> p tt m t", tt=4, t=4),
+                in_=gp[a, q][:].rearrange("p t (m tt) -> p tt m t", tt=4),
+            )
+
+        def gram_quant(a, q):
+            gq[a, q] = codes("gq%d%d" % (a, q))
+            nc.vector.quantize_mx(out=gq[a, q][0].bitcast(FP8X4), scales=gq[a, q][1], in_=ggrp[a, q][:])
+
+        def turn(src):
+            b = bank()
+            bv = b[:].rearrange("p (g u r) -> p g u r", g=2, u=2)
+            words = src.bitcast(F32)
+            for a in range(2):
+                for u in range(2):
+                    nc.tensor.transpose(bv[:, a, u, :], words[:, 256 * a + u : 256 * a + 256 : 2], ident[:])
+            return bv
+
+        def unload(bv, dst, j):
+            d = dst[:].bitcast(F32)[:, :, 256 * j : 256 * j + 256].rearrange("p g (r u) -> p g r u", u=2)
+            nc.scalar.copy(out=d, in_=bv.rearrange("p g u r -> p g r u"))
+
+        def grouped_pair():
+            t_ = work.tile([P, 2, 2048], BF16, name="pair", tag="pair", bufs=4, align_bytes=64)
+            return t_
+
+        def quant_pair(t_, label):
+            c = keep.tile([P, 2, 512], U32, name=label + "_c", align_bytes=64)
+            sc = keep.tile([P, 2, 512], U8, name=label + "_s", align_bytes=64)
+            nc.vector.quantize_mx(
+                out=c[:].rearrange("p a n -> p (a n)").bitcast(FP8X4),
+                scales=sc[:].rearrange("p a n -> p (a n)"),
+                in_=t_[:].rearrange("p a n -> p (a n)"),
+            )
+            return [(c[:, a, :], sc[:, a, :]) for a in range(2)]
+
+        sx = {}
+
+        def sx_tile(i):
+            t_ = work.tile([P, N], F32, name="sx", tag="sx", bufs=6)
+            sx[i] = t_
+            if i not in DIAG:
+                nc.vector.tensor_tensor(out=t_[:], in0=xt[i][:], in1=s_b[:], op=ALU.mult)
+                return
+            h, j = divmod(i, 4)
+            for a in range(2):
+                b = bank()
+                bv = b[:].rearrange("p (t m) -> p t m", t=4)
+                rows = xg[h][:, a, 512 * j : 512 * j + 512].rearrange("p (r t) -> p t r", t=4)
+                for t in range(4):
+                    nc.tensor.matmul(bv[:, t, :], lhsT=rows[:, t, :], rhs=diag[:, 4 * a + t, :], start=True, stop=True)
+                nc.scalar.copy(
+                    out=t_[:, 512 * a : 512 * a + 512].rearrange("p (m t) -> p m t", t=4),
+                    in_=bv.rearrange("p t m -> p m t"),
+                )
+
+        vp = {}
+
+        def vp_pair(k):
+            t_ = work.tile([P, 2, R], BF16, name="vp", tag="vp", bufs=2, align_bytes=64)
+            nc.vector.tensor_tensor(
+                out=t_[:], in0=vt[k][:], in1=g_b[:].unsqueeze(1).to_broadcast([P, 2, R]), op=ALU.mult
+            )
+            vp[2 * k] = t_[:, 0, :]
+            vp[2 * k + 1] = t_[:, 1, :]
+
+        hbank = {}
+
+        def turn_h(h, q):
+            for u in range(2):
+                b = bank()
+                hbank[h, q, u] = b
+                for j in range(4):
+                    words = ht[4 * h + j][:].bitcast(F32)
+                    nc.tensor.transpose(
+                        b[:, P * j : P * j + P], words[:, 256 * q + u : 256 * q + 256 : 2], ident[:]
+                    )
+
+        gh = {}
+
+        def unload_h(h, q):
+            t_ = work.tile([P, 4, 512], F32, name="gh", tag="gh", bufs=3)
+            gh[h, q] = t_
+            for u in range(2):
+                bv = hbank[h, q, u][:].bitcast(BF16).rearrange("p (r e) -> p e r", e=2)
+                for e in range(2):
+                    k = 4 * q + 2 * u + e
+                    nc.scalar.activation(
+                        out=t_[:, 2 * u + e, :], in_=bv[:, e, :], func=ACT.Copy, scale=gpos[:, k : k + 1]
+                    )
+
+        gxb = {}
+
+        def mm1(h, q, t):
+            b = bank()
+            gxb[h, q, t] = b
+            for a in range(2):
+                nc.tensor.matmul_mx(
+                    out=b[:],
+                    lhsT=gq[a, q][0][:, P * t : P * t + P].bitcast(FP8X4),
+                    lhsT_scale=gq[a, q][1][:, P * t : P * t + P],
+                    rhs=xq[h][a][0].bitcast(FP8X4),
+                    rhs_scale=xq[h][a][1],
+                    start=(a == 0),
+                    stop=(a == 1),
+                )
+
+        cgp = {}
+
+        def residual(h, q, t):
+            if t == 0:
+                t_ = work.tile([P, 4, 512], BF16, name="cgp", tag="cgp", bufs=2)
+                cgp[h, q] = t_
+            k = 4 * q + t
+            nc.vector.scalar_tensor_tensor(
+                out=cgp[h, q][:, t, :],
+                in0=gxb[h, q, t][:],
+                scalar=gneg[:, k : k + 1],
+                in1=gh[h, q][:, t, :],
+                op0=ALU.mult,
+                op1=ALU.add,
+            )
+
+        rgrp = {}
+
+        def r_interleave(h, q, engine):
+            t_ = work.tile([P, 2048], BF16, name="grp", tag="grp", bufs=3, align_bytes=64)
+            rgrp[h, q] = t_
+            o = t_[:].rearrange("p (c t) -> p c t", t=4)
+            i_ = cgp[h, q][:].rearrange("p t c -> p c t")
+            if engine == "act":
+                nc.scalar.copy(out=o, in_=i_)
+            else:
+                nc.vector.tensor_copy(out=o, in_=i_)
+
+        cq = {}
+
+        def r_quant(h, q):
+            c = codes("rq%d%d" % (h, q))
+            cq[h, q] = c
+            nc.vector.quantize_mx(out=c[0].bitcast(FP8X4), scales=c[1], in_=rgrp[h, q][:])
+
+        pb = {}
+
+        def mm2(i, nh, part):
+            h, j = divmod(i, 4)
+            if part == 0:
+                pb[i, nh] = bank()
+            for k, grp in enumerate((2, 3) if part == 0 else (0, 1)):
+                nc.tensor.matmul_mx(
+                    out=pb[i, nh][:],
+                    lhsT=cq[h, grp][0][:, P * j : P * j + P].bitcast(FP8X4),
+                    lhsT_scale=cq[h, grp][1][:, P * j : P * j + P],
+                    rhs=w_sb[:, grp, 1024 * nh : 1024 * nh + 1024].bitcast(FP4X4),
+                    rhs_scale=ws[:, grp, 512 * nh : 512 * nh + 512],
+                    start=(part == 0 and k == 0),
+                    stop=(part == 1 and k == 1),
+                )
+
+        def finish(i, nh):
+            c = slice(512 * nh, 512 * nh + 512)
+            nc.vector.tensor_tensor(out=sx[i][:, c], in0=sx[i][:, c], in1=pb[i, nh][:], op=ALU.add)
+
+        def clip(i, engine, c=slice(0, N)):
+            engine.tensor_scalar(
+                out=sx[i][:, c], in0=sx[i][:, c], scalar1=-1.0, scalar2=1.0, op0=ALU.max, op1=ALU.min
+            )
+
+        def store(i, c=slice(0, N)):
+            nc.sync.dma_start(out=out[P * i : P * i + P, c], in_=sx[i][:, c])
+
+        xb, xg, xq, vb, vg = {}, {}, {}, {}, {}
+
+        def x_turn(i):
+            xb[i] = turn(xt[i][:])
+
+        def x_unload(i):
+            h, j = divmod(i, 4)
+            if j == 0:
+                xg[h] = grouped_pair()
+            unload(xb[i], xg[h], j)
+
+        def v_turn(i):
+            vb[i] = turn(vp[i])
+
+        def v_unload(i):
+            h, j = divmod(i, 4)
+            if j == 0:
+                vg[h] = grouped_pair()
+            unload(vb[i], vg[h], j)
+
+        def v_quant(h):
+            c = quant_pair(vg[h], "vq%d" % h)
+            cq[h, 2] = c[0]
+            cq[h, 3] = c[1]
+
+        gram_scale_cols(0, 0)
+        for i in range(4):
+            x_turn(i)
+        x_unload(0)
+        sx_tile(0)
+        x_unload(1)
+        gram_interleave(0, 0)
+        gram_scale_cols(0, 1)
+        sx_tile(1)
+        x_unload(2)
+        x_unload(3)
+        gram_quant(0, 0)
+        gram_interleave(0, 1)
+        nc.vector.tensor_copy(out=gpos[:], in_=gcol[:])
+        nc.vector.tensor_scalar(out=gneg[:], in0=gcol[:], scalar1=-1.0, scalar2=None, op0=ALU.mult)
+        xq[0] = quant_pair(xg[0], "xq0")
+        gram_scale_cols(1, 0)
+        gram_quant(0, 1)
+        for i in range(4, 8):
+            x_turn(i)
+        gram_interleave(1, 0)
+        gram_scale_cols(1, 1)
+        turn_h(0, 0)
+        unload_h(0, 0)
+        gram_quant(1, 0)
+        gram_interleave(1, 1)
+        for t in range(4):
+            mm1(0, 0, t)
+        gram_quant(1, 1)
+        turn_h(0, 1)
+        for t in range(4):
+            residual(0, 0, t)
+        unload_h(0, 1)
+        for t in range(4):
+            mm1(0, 1, t)
+        r_interleave(0, 0, "act")
+        for i in range(4, 8):
+            x_unload(i)
+        vp_pair(0)
+        vp_pair(1)
+        for t in range(4):
+            residual(0, 1, t)
+        xq[1] = quant_pair(xg[1], "xq1")
+        r_quant(0, 0)
+        for i in range(4):
+            v_turn(i)
+        r_interleave(0, 1, "act")
+        for i in range(4):
+            v_unload(i)
+        v_quant(0)
+        r_quant(0, 1)
+        vp_pair(2)
+        vp_pair(3)
+        turn_h(1, 0)
+        unload_h(1, 0)
+        for t in range(4):
+            mm1(1, 0, t)
+        for t in range(4):
+            residual(1, 0, t)
+        turn_h(1, 1)
+        unload_h(1, 1)
+        r_interleave(1, 0, "act")
+        for t in range(4):
+            mm1(1, 1, t)
+        sx_tile(2)
+        for t in range(4):
+            residual(1, 1, t)
+        r_interleave(1, 1, "act")
+        for i in range(4, 8):
+            v_turn(i)
+        for i in range(4, 8):
+            v_unload(i)
+        for i in range(8):
+            if i == 2:
+                v_quant(1)
+                r_quant(1, 0)
+            if i == 3:
+                r_quant(1, 1)
+            if 1 <= i < 6:
+                sx_tile(i + 2)
+            for nh in range(2):
+                mm2(i, nh, 0)
+                mm2(i, nh, 1)
+                finish(i, nh)
+                if i == 7:
+                    c = slice(512 * nh, 512 * nh + 512)
+                    clip(i, nc.vector, c)
+                    store(i, c)
+            if i < 7:
+                clip(i, nc.gpsimd if i < 6 else nc.vector)
+                store(i)

@@ -30,7 +30,7 @@ def tile_clippedlinearresidualupdate_kernel(
         s_b = keep.tile([P, N], BF16, name="s_b")
         gcol = keep.tile([P, 8], BF16, name="gcol")
         scol = keep.tile([P, 8], BF16, name="scol")
-        g_b = keep.tile([P, R], BF16, name="g_b")
+        g_b = keep.tile([P, 2, R], BF16, name="g_b")
         gview = gram_bytes.rearrange("(g p t) n -> g p t n", p=P, t=4)
         graw = []
         for a in range(2):
@@ -56,7 +56,7 @@ def tile_clippedlinearresidualupdate_kernel(
         nc.sync.dma_start(out=graw[1][:], in_=gview[1])
         load_rows(x, "x", xt, range(4, 8))
         load_rows(hty, "h", ht, range(8))
-        nc.sync.dma_start(out=g_b[:], in_=g[R : 2 * R].partition_broadcast(P))
+        nc.sync.dma_start(out=g_b[:, 0, :], in_=g[R : 2 * R].partition_broadcast(P))
         for i in range(4):
             t_ = keep.tile([P, 2, R], BF16, name="v%d" % i, align_bytes=64)
             nc.sync.dma_start(out=t_[:], in_=v[2 * P * i : 2 * P * i + 2 * P, :].rearrange("(i p) n -> p i n", p=P))
@@ -127,13 +127,14 @@ def tile_clippedlinearresidualupdate_kernel(
             gq[a, q] = codes("gq%d%d" % (a, q))
             nc.vector.quantize_mx(out=gq[a, q][0].bitcast(FP8X4), scales=gq[a, q][1], in_=ggrp[a, q][:])
 
-        def turn(src):
+        def turn(src, stepped):
             b = bank()
             bv = b[:].rearrange("p (g u r) -> p g u r", g=2, u=2)
             words = src.bitcast(F32)
             for a in range(2):
                 for u in range(2):
-                    nc.tensor.transpose(bv[:, a, u, :], words[:, 256 * a + u : 256 * a + 256 : 2], ident[:])
+                    w = words[:, 256 * a + u : 256 * a + 256 : 2] if stepped else words[:, a, u, :]
+                    nc.tensor.transpose(bv[:, a, u, :], w, ident[:])
             return bv
 
         def unload(bv, dst, j):
@@ -177,12 +178,17 @@ def tile_clippedlinearresidualupdate_kernel(
         vp = {}
 
         def vp_pair(k):
-            t_ = work.tile([P, 2, R], BF16, name="vp", tag="vp", bufs=2, align_bytes=64)
-            nc.vector.tensor_tensor(
-                out=t_[:], in0=vt[k][:], in1=g_b[:].unsqueeze(1).to_broadcast([P, 2, R]), op=ALU.mult
-            )
-            vp[2 * k] = t_[:, 0, :]
-            vp[2 * k + 1] = t_[:, 1, :]
+            t_ = work.tile([P, 4, 2, 256], BF16, name="vp", tag="vp", bufs=2, align_bytes=64)
+            if k == 0:
+                nc.vector.tensor_copy(out=g_b[:, 1, :], in_=g_b[:, 0, :])
+            v4 = vt[k][:].rearrange("p i (a w u e) -> p u (i a) w e", a=2, u=2, e=2)
+            g4 = g_b[:].rearrange("p i (a w u e) -> p u (i a) w e", a=2, u=2, e=2)
+            for u in range(2):
+                nc.vector.tensor_tensor(
+                    out=t_[:, :, u, :].rearrange("p c (w e) -> p c w e", e=2), in0=v4[:, u], in1=g4[:, u], op=ALU.mult
+                )
+            vp[2 * k] = t_[:, 0:2]
+            vp[2 * k + 1] = t_[:, 2:4]
 
         hbank = {}
 
@@ -292,7 +298,7 @@ def tile_clippedlinearresidualupdate_kernel(
         xb, xg, xq, vb, vg = {}, {}, {}, {}, {}
 
         def x_turn(i):
-            xb[i] = turn(xt[i][:])
+            xb[i] = turn(xt[i][:], True)
 
         def x_unload(i):
             h, j = divmod(i, 4)
@@ -301,7 +307,7 @@ def tile_clippedlinearresidualupdate_kernel(
             unload(xb[i], xg[h], j)
 
         def v_turn(i):
-            vb[i] = turn(vp[i])
+            vb[i] = turn(vp[i], False)
 
         def v_unload(i):
             h, j = divmod(i, 4)
@@ -403,5 +409,5 @@ def tile_clippedlinearresidualupdate_kernel(
                     clip(i, nc.vector, c)
                     store(i, c)
             if i < 7:
-                clip(i, nc.gpsimd if i < 6 else nc.vector)
+                clip(i, nc.vector)
                 store(i)

@@ -15,6 +15,7 @@ FP4X4 = mybir.dt.float4_e2m1fn_x4
 ALU = mybir.AluOpType
 ACT = mybir.ActivationFunctionType
 P = 128
+GRAM_ON_VECTOR = {(0, 0): (2, 3), (0, 1): (3,), (1, 0): (3,), (1, 1): (3,)}
 DIAG = (4, 5, 6, 7)
 
 
@@ -44,19 +45,25 @@ def tile_clippedlinearresidualupdate_kernel(
                 tiles.append(t_)
 
         xt, ht, vt = [], [], []
-        nc.sync.dma_start(out=graw[0][:], in_=gview[0])
-        nc.scalar.dma_start(
+        rows = keep.tile([P, 2 * N], BF16, name="rows", align_bytes=64)
+        nc.vector.memset(rows[:].bitcast(I32), 0)
+        ones = keep.tile([P, P], BF16, name="ones")
+        nc.vector.memset(ones[:], 1.0)
+        nc.scalar.dma_start(out=rows[0:1, 0:N], in_=s.unsqueeze(0))
+        nc.scalar.dma_start(out=rows[0:1, N : 2 * N], in_=g[R : 2 * R].unsqueeze(0))
+        for q in range(2):
+            c = slice(512 * q, 512 * q + 512)
+            nc.sync.dma_start(out=graw[0][:, :, c], in_=gview[0][:, :, c])
+            load_rows(x, "x", xt, range(2 * q, 2 * q + 2))
+        nc.sync.dma_start(out=graw[1][:], in_=gview[1])
+        nc.sync.dma_start(
             out=gcol[:].rearrange("p (q t) -> p q t", t=4), in_=g[0:R].rearrange("(q p t) -> p q t", p=P, t=4)
         )
-        nc.scalar.dma_start(
+        load_rows(x, "x", xt, range(4, 8))
+        load_rows(hty, "h", ht, range(0, 8))
+        nc.sync.dma_start(
             out=scol[:].rearrange("p (q t) -> p q t", t=4), in_=s.rearrange("(q p t) -> p q t", p=P, t=4)
         )
-        nc.scalar.dma_start(out=s_b[:], in_=s.partition_broadcast(P))
-        load_rows(x, "x", xt, range(4))
-        nc.sync.dma_start(out=graw[1][:], in_=gview[1])
-        load_rows(x, "x", xt, range(4, 8))
-        load_rows(hty, "h", ht, range(8))
-        nc.sync.dma_start(out=g_b[:, 0, :], in_=g[R : 2 * R].partition_broadcast(P))
         for i in range(4):
             t_ = keep.tile([P, 2, R], BF16, name="v%d" % i, align_bytes=64)
             nc.sync.dma_start(out=t_[:], in_=v[2 * P * i : 2 * P * i + 2 * P, :].rearrange("(i p) n -> p i n", p=P))
@@ -96,6 +103,15 @@ def tile_clippedlinearresidualupdate_kernel(
             b = psum.tile([P, 512], F32, name="bank", tag="bank")
             return b
 
+        def spread(dst, lo, eng):
+            for k in range(2):
+                b = bank()
+                nc.tensor.matmul(b[:], lhsT=ones[:], rhs=rows[:, lo + 512 * k : lo + 512 * k + 512], start=True, stop=True)
+                if eng == "act":
+                    nc.scalar.copy(out=dst[:, 512 * k : 512 * k + 512], in_=b[:])
+                else:
+                    nc.vector.tensor_copy(out=dst[:, 512 * k : 512 * k + 512], in_=b[:])
+
         gp = {}
         ggrp = {}
         gq = {}
@@ -110,7 +126,7 @@ def tile_clippedlinearresidualupdate_kernel(
                     o = t_[:, t, P * j : P * j + P]
                     i_ = graw[a][:, t, col : col + P].bitcast(FP8)
                     sc = gsc[:, a, k : k + 1]
-                    if a == 0 and q == 0 and t >= 2:
+                    if t in GRAM_ON_VECTOR[a, q]:
                         nc.vector.tensor_scalar(out=o, in0=i_, scalar1=sc, scalar2=None, op0=ALU.mult)
                     else:
                         nc.scalar.activation(out=o, in_=i_, func=ACT.Copy, scale=sc)
@@ -179,8 +195,6 @@ def tile_clippedlinearresidualupdate_kernel(
 
         def vp_pair(k):
             t_ = work.tile([P, 4, 2, 256], BF16, name="vp", tag="vp", bufs=2, align_bytes=64)
-            if k == 0:
-                nc.vector.tensor_copy(out=g_b[:, 1, :], in_=g_b[:, 0, :])
             v4 = vt[k][:].rearrange("p i (a w u e) -> p u (i a) w e", a=2, u=2, e=2)
             g4 = g_b[:].rearrange("p i (a w u e) -> p u (i a) w e", a=2, u=2, e=2)
             for u in range(2):
@@ -320,6 +334,7 @@ def tile_clippedlinearresidualupdate_kernel(
             cq[h, 2] = c[0]
             cq[h, 3] = c[1]
 
+        spread(s_b, 0, "dve")
         gram_scale_cols(0, 0)
         for i in range(4):
             x_turn(i)
@@ -341,6 +356,8 @@ def tile_clippedlinearresidualupdate_kernel(
         for i in range(4, 8):
             x_turn(i)
         gram_interleave(1, 0)
+        spread(g_b[:, 0, :], N, "act")
+        nc.vector.tensor_copy(out=g_b[:, 1, :], in_=g_b[:, 0, :])
         gram_scale_cols(1, 1)
         turn_h(0, 0)
         unload_h(0, 0)

@@ -266,8 +266,8 @@ def tile_clippedlinearresidualupdate_kernel(
         def r_interleave(h, q, engine):
             t_ = work.tile([P, 2048], BF16, name="grp", tag="grp", bufs=3, align_bytes=64)
             rgrp[h, q] = t_
-            o = t_[:].rearrange("p (c t) -> p c t", t=4)
-            i_ = cgp[h, q][:].rearrange("p t c -> p c t")
+            o = t_[:].rearrange("p (c i t) -> p c t i", i=4, t=4)
+            i_ = cgp[h, q][:].rearrange("p t (c i) -> p c t i", i=4)
             if engine == "act":
                 nc.scalar.copy(out=o, in_=i_)
             else:

import concourse.mybir as mybir
from concourse.masks import make_identity

B, N, R = 1024, 1024, 1024
FLOPS = 2 * B * N * R + 2 * B * (2 * R) * N

F32 = mybir.dt.float32
BF16 = mybir.dt.bfloat16
I32 = mybir.dt.int32
U32 = mybir.dt.uint32
U8 = mybir.dt.uint8
FP8 = mybir.dt.float8_e4m3fn
FP8X4 = mybir.dt.float8_e4m3fn_x4
FP4X4 = mybir.dt.float4_e2m1fn_x4
ALU = mybir.AluOpType
ACT = mybir.ActivationFunctionType
P = 128
GRAM_ON_VECTOR = {(0, 0): (2, 3), (0, 1): (3,), (1, 0): (3,), (1, 1): (3,)}
DIAG = (4, 5, 6, 7)


def tile_clippedlinearresidualupdate_kernel(
    tc, x, v, hty, gram_bytes, gram_scale, g, w_words, w_scales, s, out
):
    nc = tc.nc
    with tc.tile_pool(name="keep", bufs=1) as keep, tc.tile_pool(name="work", bufs=2) as work, tc.psum_pool(
        name="psum", bufs=8
    ) as psum:
        gsc = keep.tile([P, 2, 32], F32, name="gsc")
        nc.sync.dma_start(out=gsc[:], in_=gram_scale.rearrange("(g p t) j -> p g (t j)", p=P, t=4))
        s_b = keep.tile([P, N], BF16, name="s_b")
        gcol = keep.tile([P, 8], BF16, name="gcol")
        scol = keep.tile([P, 8], BF16, name="scol")
        g_b = keep.tile([P, 2, R], BF16, name="g_b")
        gview = gram_bytes.rearrange("(g p t) n -> g p t n", p=P, t=4)
        graw = []
        for a in range(2):
            t_ = keep.tile([P, 4, N], U8, name="gram_raw%d" % a)
            graw.append(t_)

        def load_rows(src, label, tiles, rows):
            for i in rows:
                t_ = keep.tile([P, 1024], BF16, name="%s%d" % (label, i), align_bytes=64)
                nc.sync.dma_start(out=t_[:], in_=src[P * i : P * i + P, :])
                tiles.append(t_)

        xt, ht, vt = [], [], []
        rows = keep.tile([P, 2 * N], BF16, name="rows", align_bytes=64)
        nc.vector.memset(rows[:].bitcast(I32), 0)
        ones = keep.tile([P, P], BF16, name="ones")
        nc.vector.memset(ones[:], 1.0)
        nc.scalar.dma_start(out=rows[0:1, 0:N], in_=s.unsqueeze(0))
        nc.scalar.dma_start(out=rows[0:1, N : 2 * N], in_=g[R : 2 * R].unsqueeze(0))
        for q in range(2):
            c = slice(512 * q, 512 * q + 512)
            nc.sync.dma_start(out=graw[0][:, :, c], in_=gview[0][:, :, c])
            load_rows(x, "x", xt, range(2 * q, 2 * q + 2))
        nc.sync.dma_start(out=graw[1][:], in_=gview[1])
        nc.sync.dma_start(
            out=gcol[:].rearrange("p (q t) -> p q t", t=4), in_=g[0:R].rearrange("(q p t) -> p q t", p=P, t=4)
        )
        load_rows(x, "x", xt, range(4, 8))
        load_rows(hty, "h", ht, range(0, 8))
        nc.sync.dma_start(
            out=scol[:].rearrange("p (q t) -> p q t", t=4), in_=s.rearrange("(q p t) -> p q t", p=P, t=4)
        )
        for i in range(4):
            t_ = keep.tile([P, 2, R], BF16, name="v%d" % i, align_bytes=64)
            nc.sync.dma_start(out=t_[:], in_=v[2 * P * i : 2 * P * i + 2 * P, :].rearrange("(i p) n -> p i n", p=P))
            vt.append(t_)

        ident = keep.tile([P, P], F32, name="ident")
        make_identity(nc, ident[:])
        ident_b = keep.tile([P, P], BF16, name="ident_b")
        make_identity(nc, ident_b[:])
        diag = keep.tile([P, 8, P], BF16, name="diag")
        nc.gpsimd.tensor_tensor(
            out=diag[:],
            in0=ident_b[:].unsqueeze(1).to_broadcast([P, 8, P]),
            in1=scol[:].unsqueeze(2).to_broadcast([P, 8, P]),
            op=ALU.mult,
        )
        ws = keep.tile([P, 4, N], U8, name="ws", align_bytes=64)
        nc.gpsimd.memset(ws[:].bitcast(I32), 0)

        w_sb = keep.tile([P, 4, 2 * N], U8, name="w_sb", align_bytes=64)
        nc.sync.dma_start(out=w_sb[:], in_=w_words.rearrange("g p c -> p g c"))
        for q in range(4):
            nc.sync.dma_start(
                out=ws[32 * q : 32 * q + 4, :, :].bitcast(I32),
                in_=w_scales[:, 4 * q : 4 * q + 4, :].rearrange("g r n -> r g n").bitcast(I32),
            )

        gpos = keep.tile([P, 8], F32, name="gpos")
        gneg = keep.tile([P, 8], F32, name="gneg")

        def codes(label):
            c = keep.tile([P, 512], U32, name=label + "_c", align_bytes=64)
            sc = keep.tile([P, 512], U8, name=label + "_s", align_bytes=64)
            return c[:], sc[:]

        def bank():
            b = psum.tile([P, 512], F32, name="bank", tag="bank")
            return b

        def spread(dst, lo, eng):
            for k in range(2):
                b = bank()
                nc.tensor.matmul(b[:], lhsT=ones[:], rhs=rows[:, lo + 512 * k : lo + 512 * k + 512], start=True, stop=True)
                if eng == "act":
                    nc.scalar.copy(out=dst[:, 512 * k : 512 * k + 512], in_=b[:])
                else:
                    nc.vector.tensor_copy(out=dst[:, 512 * k : 512 * k + 512], in_=b[:])

        gp = {}
        ggrp = {}
        gq = {}

        def gram_scale_cols(a, q):
            t_ = work.tile([P, 4, 512], BF16, name="gp", tag="gp", bufs=2)
            gp[a, q] = t_
            for j in range(4):
                for t in range(4):
                    col = 512 * q + P * j
                    k = 8 * t + 4 * q + j
                    o = t_[:, t, P * j : P * j + P]
                    i_ = graw[a][:, t, col : col + P].bitcast(FP8)
                    sc = gsc[:, a, k : k + 1]
                    if t in GRAM_ON_VECTOR[a, q]:
                        nc.vector.tensor_scalar(out=o, in0=i_, scalar1=sc, scalar2=None, op0=ALU.mult)
                    else:
                        nc.scalar.activation(out=o, in_=i_, func=ACT.Copy, scale=sc)

        def gram_interleave(a, q):
            t_ = work.tile([P, 2048], BF16, name="grp", tag="grp", bufs=3, align_bytes=64)
            ggrp[a, q] = t_
            nc.vector.tensor_copy(
                out=t_[:].rearrange("p (tt m t) -> p tt m t", tt=4, t=4),
                in_=gp[a, q][:].rearrange("p t (m tt) -> p tt m t", tt=4),
            )

        def gram_quant(a, q):
            gq[a, q] = codes("gq%d%d" % (a, q))
            nc.vector.quantize_mx(out=gq[a, q][0].bitcast(FP8X4), scales=gq[a, q][1], in_=ggrp[a, q][:])

        def turn(src, stepped):
            b = bank()
            bv = b[:].rearrange("p (g u r) -> p g u r", g=2, u=2)
            words = src.bitcast(F32)
            for a in range(2):
                for u in range(2):
                    w = words[:, 256 * a + u : 256 * a + 256 : 2] if stepped else words[:, a, u, :]
                    nc.tensor.transpose(bv[:, a, u, :], w, ident[:])
            return bv

        def unload(bv, dst, j):
            d = dst[:].bitcast(F32)[:, :, 256 * j : 256 * j + 256].rearrange("p g (r u) -> p g r u", u=2)
            nc.scalar.copy(out=d, in_=bv.rearrange("p g u r -> p g r u"))

        def grouped_pair():
            t_ = work.tile([P, 2, 2048], BF16, name="pair", tag="pair", bufs=4, align_bytes=64)
            return t_

        def quant_pair(t_, label):
            c = keep.tile([P, 2, 512], U32, name=label + "_c", align_bytes=64)
            sc = keep.tile([P, 2, 512], U8, name=label + "_s", align_bytes=64)
            nc.vector.quantize_mx(
                out=c[:].rearrange("p a n -> p (a n)").bitcast(FP8X4),
                scales=sc[:].rearrange("p a n -> p (a n)"),
                in_=t_[:].rearrange("p a n -> p (a n)"),
            )
            return [(c[:, a, :], sc[:, a, :]) for a in range(2)]

        sx = {}

        def sx_tile(i):
            t_ = work.tile([P, N], F32, name="sx", tag="sx", bufs=6)
            sx[i] = t_
            if i not in DIAG:
                nc.vector.tensor_tensor(out=t_[:], in0=xt[i][:], in1=s_b[:], op=ALU.mult)
                return
            h, j = divmod(i, 4)
            for a in range(2):
                b = bank()
                bv = b[:].rearrange("p (t m) -> p t m", t=4)
                rows = xg[h][:, a, 512 * j : 512 * j + 512].rearrange("p (r t) -> p t r", t=4)
                for t in range(4):
                    nc.tensor.matmul(bv[:, t, :], lhsT=rows[:, t, :], rhs=diag[:, 4 * a + t, :], start=True, stop=True)
                nc.scalar.copy(
                    out=t_[:, 512 * a : 512 * a + 512].rearrange("p (m t) -> p m t", t=4),
                    in_=bv.rearrange("p t m -> p m t"),
                )

        vp = {}

        def vp_pair(k):
            t_ = work.tile([P, 4, 2, 256], BF16, name="vp", tag="vp", bufs=2, align_bytes=64)
            v4 = vt[k][:].rearrange("p i (a w u e) -> p u (i a) w e", a=2, u=2, e=2)
            g4 = g_b[:].rearrange("p i (a w u e) -> p u (i a) w e", a=2, u=2, e=2)
            for u in range(2):
                nc.vector.tensor_tensor(
                    out=t_[:, :, u, :].rearrange("p c (w e) -> p c w e", e=2), in0=v4[:, u], in1=g4[:, u], op=ALU.mult
                )
            vp[2 * k] = t_[:, 0:2]
            vp[2 * k + 1] = t_[:, 2:4]

        hbank = {}

        def turn_h(h, q):
            for u in range(2):
                b = bank()
                hbank[h, q, u] = b
                for j in range(4):
                    words = ht[4 * h + j][:].bitcast(F32)
                    nc.tensor.transpose(
                        b[:, P * j : P * j + P], words[:, 256 * q + u : 256 * q + 256 : 2], ident[:]
                    )

        gh = {}

        def unload_h(h, q):
            t_ = work.tile([P, 4, 512], F32, name="gh", tag="gh", bufs=3)
            gh[h, q] = t_
            for u in range(2):
                bv = hbank[h, q, u][:].bitcast(BF16).rearrange("p (r e) -> p e r", e=2)
                for e in range(2):
                    k = 4 * q + 2 * u + e
                    nc.scalar.activation(
                        out=t_[:, 2 * u + e, :], in_=bv[:, e, :], func=ACT.Copy, scale=gpos[:, k : k + 1]
                    )

        gxb = {}

        def mm1(h, q, t):
            b = bank()
            gxb[h, q, t] = b
            for a in range(2):
                nc.tensor.matmul_mx(
                    out=b[:],
                    lhsT=gq[a, q][0][:, P * t : P * t + P].bitcast(FP8X4),
                    lhsT_scale=gq[a, q][1][:, P * t : P * t + P],
                    rhs=xq[h][a][0].bitcast(FP8X4),
                    rhs_scale=xq[h][a][1],
                    start=(a == 0),
                    stop=(a == 1),
                )

        cgp = {}

        def residual(h, q, t):
            if t == 0:
                t_ = work.tile([P, 4, 512], BF16, name="cgp", tag="cgp", bufs=2)
                cgp[h, q] = t_
            k = 4 * q + t
            nc.vector.scalar_tensor_tensor(
                out=cgp[h, q][:, t, :],
                in0=gxb[h, q, t][:],
                scalar=gneg[:, k : k + 1],
                in1=gh[h, q][:, t, :],
                op0=ALU.mult,
                op1=ALU.add,
            )

        rgrp = {}

        def r_interleave(h, q, engine):
            t_ = work.tile([P, 2048], BF16, name="grp", tag="grp", bufs=3, align_bytes=64)
            rgrp[h, q] = t_
            o = t_[:].rearrange("p (c i t) -> p c t i", i=4, t=4)
            i_ = cgp[h, q][:].rearrange("p t (c i) -> p c t i", i=4)
            if engine == "act":
                nc.scalar.copy(out=o, in_=i_)
            else:
                nc.vector.tensor_copy(out=o, in_=i_)

        cq = {}

        def r_quant(h, q):
            c = codes("rq%d%d" % (h, q))
            cq[h, q] = c
            nc.vector.quantize_mx(out=c[0].bitcast(FP8X4), scales=c[1], in_=rgrp[h, q][:])

        pb = {}

        def mm2(i, nh, part):
            h, j = divmod(i, 4)
            if part == 0:
                pb[i, nh] = bank()
            for k, grp in enumerate((2, 3) if part == 0 else (0, 1)):
                nc.tensor.matmul_mx(
                    out=pb[i, nh][:],
                    lhsT=cq[h, grp][0][:, P * j : P * j + P].bitcast(FP8X4),
                    lhsT_scale=cq[h, grp][1][:, P * j : P * j + P],
                    rhs=w_sb[:, grp, 1024 * nh : 1024 * nh + 1024].bitcast(FP4X4),
                    rhs_scale=ws[:, grp, 512 * nh : 512 * nh + 512],
                    start=(part == 0 and k == 0),
                    stop=(part == 1 and k == 1),
                )

        def finish(i, nh):
            c = slice(512 * nh, 512 * nh + 512)
            nc.vector.tensor_tensor(out=sx[i][:, c], in0=sx[i][:, c], in1=pb[i, nh][:], op=ALU.add)

        def clip(i, engine, c=slice(0, N)):
            engine.tensor_scalar(
                out=sx[i][:, c], in0=sx[i][:, c], scalar1=-1.0, scalar2=1.0, op0=ALU.max, op1=ALU.min
            )

        def store(i, c=slice(0, N)):
            nc.sync.dma_start(out=out[P * i : P * i + P, c], in_=sx[i][:, c])

        xb, xg, xq, vb, vg = {}, {}, {}, {}, {}

        def x_turn(i):
            xb[i] = turn(xt[i][:], True)

        def x_unload(i):
            h, j = divmod(i, 4)
            if j == 0:
                xg[h] = grouped_pair()
            unload(xb[i], xg[h], j)

        def v_turn(i):
            vb[i] = turn(vp[i], False)

        def v_unload(i):
            h, j = divmod(i, 4)
            if j == 0:
                vg[h] = grouped_pair()
            unload(vb[i], vg[h], j)

        def v_quant(h):
            c = quant_pair(vg[h], "vq%d" % h)
            cq[h, 2] = c[0]
            cq[h, 3] = c[1]

        spread(s_b, 0, "dve")
        gram_scale_cols(0, 0)
        for i in range(4):
            x_turn(i)
        x_unload(0)
        sx_tile(0)
        x_unload(1)
        gram_interleave(0, 0)
        gram_scale_cols(0, 1)
        sx_tile(1)
        x_unload(2)
        x_unload(3)
        gram_quant(0, 0)
        gram_interleave(0, 1)
        nc.vector.tensor_copy(out=gpos[:], in_=gcol[:])
        nc.vector.tensor_scalar(out=gneg[:], in0=gcol[:], scalar1=-1.0, scalar2=None, op0=ALU.mult)
        xq[0] = quant_pair(xg[0], "xq0")
        gram_scale_cols(1, 0)
        gram_quant(0, 1)
        for i in range(4, 8):
            x_turn(i)
        gram_interleave(1, 0)
        spread(g_b[:, 0, :], N, "act")
        nc.vector.tensor_copy(out=g_b[:, 1, :], in_=g_b[:, 0, :])
        gram_scale_cols(1, 1)
        turn_h(0, 0)
        unload_h(0, 0)
        gram_quant(1, 0)
        gram_interleave(1, 1)
        for t in range(4):
            mm1(0, 0, t)
        gram_quant(1, 1)
        turn_h(0, 1)
        for t in range(4):
            residual(0, 0, t)
        unload_h(0, 1)
        for t in range(4):
            mm1(0, 1, t)
        r_interleave(0, 0, "act")
        for i in range(4, 8):
            x_unload(i)
        vp_pair(0)
        vp_pair(1)
        for t in range(4):
            residual(0, 1, t)
        xq[1] = quant_pair(xg[1], "xq1")
        r_quant(0, 0)
        for i in range(4):
            v_turn(i)
        r_interleave(0, 1, "act")
        for i in range(4):
            v_unload(i)
        v_quant(0)
        r_quant(0, 1)
        vp_pair(2)
        vp_pair(3)
        turn_h(1, 0)
        unload_h(1, 0)
        for t in range(4):
            mm1(1, 0, t)
        for t in range(4):
            residual(1, 0, t)
        turn_h(1, 1)
        unload_h(1, 1)
        r_interleave(1, 0, "act")
        for t in range(4):
            mm1(1, 1, t)
        sx_tile(2)
        for t in range(4):
            residual(1, 1, t)
        r_interleave(1, 1, "act")
        for i in range(4, 8):
            v_turn(i)
        for i in range(4, 8):
            v_unload(i)
        for i in range(8):
            if i == 2:
                v_quant(1)
                r_quant(1, 0)
            if i == 3:
                r_quant(1, 1)
            if 1 <= i < 6:
                sx_tile(i + 2)
            for nh in range(2):
                mm2(i, nh, 0)
                mm2(i, nh, 1)
                finish(i, nh)
                if i == 7:
                    c = slice(512 * nh, 512 * nh + 512)
                    clip(i, nc.vector, c)
                    store(i, c)
            if i < 7:
                clip(i, nc.vector)
                store(i)
